import numpy as np
import ml_dtypes


def mxq(x, axis, fmt="e4m3"):
    dtype, down = {"e4m3": (ml_dtypes.float8_e4m3fn, 7), "e5m2": (ml_dtypes.float8_e5m2, 14)}[fmt]
    v = np.moveaxis(np.asarray(x, np.float32).astype(ml_dtypes.bfloat16).astype(np.float64), axis, -1)
    blocks = v.reshape(v.shape[:-1] + (-1, 32))
    amax = np.abs(blocks).max(-1, keepdims=True)
    byte = np.maximum(np.where(amax > 0, np.frexp(amax)[1] - 1 + 127, 0) - down, 1)
    scale = np.exp2(byte - 127.0)
    codes = (blocks / scale).astype(np.float32).astype(dtype).astype(np.float64)
    return np.moveaxis((codes * scale).reshape(v.shape), -1, axis)


WIDE = False


def mx_kscale(k):
    if not WIDE:
        return np.ones(k)
    levels = np.array([10, -10, 5, -5, 0])
    if k % 512:
        return np.exp2(np.random.permutation(np.resize(levels, k // 32))).repeat(32)
    a = np.empty((k // 512, 16))
    for p in range(k // 512):
        a[p, :8] = np.random.permutation(np.resize(levels, 8))
        for g in range(8):
            far = levels[np.abs(levels - a[p, g]) >= 10]
            a[p, g + 8] = far[np.random.randint(len(far))]
    return np.exp2(a.ravel()).repeat(32)


def f64(x):
    return np.asarray(x).astype(np.float64)


def striped(idx):
    return np.tile(idx.reshape(-1, 16).T, (8, 1)).astype(np.uint16)


def unstriped(offs):
    return offs[:16].T.reshape(-1).astype(np.int64)


E2M1 = np.array([0.0, 0.5, 1.0, 1.5, 2.0, 3.0, 4.0, 6.0, -0.0, -0.5, -1.0, -1.5, -2.0, -3.0, -4.0, -6.0])


def pack_weight(w, fmt):
    k, n = w.shape
    w = f64(np.asarray(w, np.float32).astype(ml_dtypes.bfloat16)).reshape(k // 32, 32, n)
    amax = np.abs(w).max(1)
    if fmt == "e4m3":
        byte = np.frexp(amax)[1] - 1 + 127 - 7
    else:
        mant, ex = np.frexp(amax / 6.0)
        byte = np.where(mant > 0.5, ex, ex - 1) + 127
    byte = np.clip(np.where(amax > 0, byte, 1), 1, 254)
    scaled = (w * np.exp2(127.0 - byte)[:, None, :]).reshape(k, n).astype(np.float32)
    by_word = np.ascontiguousarray(scaled.reshape(k // 512, 128, 4, n).transpose(0, 1, 3, 2))
    if fmt == "e4m3":
        words = by_word.astype(ml_dtypes.float8_e4m3fn).view(np.uint8)
    else:
        c = by_word.astype(ml_dtypes.float4_e2m1fn).view(np.uint8) & 0xF
        words = (c[..., 0::2] | (c[..., 1::2] << 4)).reshape(k // 512, 128, 2 * n)
    return np.ascontiguousarray(words), np.ascontiguousarray(byte.astype(np.uint8).reshape(k // 512, 16, n))


def unpack_weight(words, scales, fmt):
    g, _, n = scales.shape
    words = np.ascontiguousarray(words).reshape(g, 128, n, -1)
    if fmt == "e4m3":
        vals = words.view(ml_dtypes.float8_e4m3fn).astype(np.float64)
    else:
        nib = np.empty((g, 128, n, 4), np.uint8)
        nib[..., 0::2] = words & 0xF
        nib[..., 1::2] = words >> 4
        vals = E2M1[nib]
    vals = vals * np.repeat(np.exp2(scales.astype(np.float64) - 127.0), 8, axis=1)[..., None]
    return vals.transpose(0, 1, 3, 2).reshape(g * 512, n)


def planes(y):
    n, m = y.shape
    v = y.astype(np.float32).astype(ml_dtypes.bfloat16).astype(np.float64).reshape(n // 32, 32, m)
    top = np.abs(v).max(1)
    byte = np.clip(np.where(top > 0, np.frexp(top)[1] - 1 + 127 - 7, 1), 1, 254)
    codes = (v * np.exp2(127.0 - byte)[:, None, :]).reshape(n, m).astype(np.float32).astype(ml_dtypes.float8_e4m3fn).view(np.uint8)
    words = codes.reshape(n // 512, 128, 4, m).transpose(0, 1, 3, 2)
    return np.ascontiguousarray(words), np.ascontiguousarray(byte.astype(np.uint8).reshape(n // 512, 16, m))


def relu(v):
    return np.maximum(v, 0.0)


def sigmoid(v):
    return 1.0 / (1.0 + np.exp(-np.maximum(v, -700.0)))


K, T, E, C, H, N, TOP = 512, 512, 8, 256, 512, 512, 4


def by_expert(wq, xq):
    return np.concatenate([wq[e].T @ xq[:, e * C:(e + 1) * C] for e in range(E)], axis=1)


def setup_inputs():
    n = np.random.standard_normal
    s = mx_kscale(K)
    u = mx_kscale(H)
    deal = np.repeat(np.arange(E), C).reshape(TOP, T)[:, np.random.permutation(T)]
    deal = np.take_along_axis(deal, np.argsort(np.random.rand(TOP, T), axis=0), axis=0)
    for _ in range(8):
        s_, t_ = np.random.permutation(T).reshape(2, -1); r = np.random.randint(TOP, size=T // 2); x, y = deal[r, s_].copy(), deal[r, t_].copy()
        ok = ~((deal[:, s_] == y).any(0) | (deal[:, t_] == x).any(0)); deal[r[ok], s_[ok]] = y[ok]; deal[r[ok], t_[ok]] = x[ok]
    order = np.argsort(deal.reshape(-1) + 0.5 * np.random.rand(TOP * T))
    slot_token = order % T; pos = np.empty(TOP * T, np.int64); pos[order] = np.arange(TOP * T); pos = pos.reshape(TOP, T)
    g = np.random.uniform(0.5, 1.5, (TOP, T)); g = g / g.sum(0)
    x = pack_weight(n((K, T)) * s[:, None], "e4m3")
    wg = pack_weight(n((K, N)) / np.sqrt(K) / s[:, None], "e2m1")
    return {
        "x_words": x[0],
        "x_scales": x[1],
        "wg_words": wg[0],
        "wg_scales": wg[1],
        "w1": (n((E, K, H)) / np.sqrt(K) / s[None, :, None] * u).astype(np.float32),
        "w2": (n((E, H, N)) / np.sqrt(H) / u[None, :, None]).astype(np.float32),
        "gate": np.stack([np.tile(r, (128, 1)) for r in g]).astype(np.float32),
        "offs": striped(slot_token),
        "pos1": striped(pos[0]),
        "pos2": striped(pos[1]),
        "pos3": striped(pos[2]),
        "pos4": striped(pos[3]),
    }


def reference(x_words, x_scales, wg_words, wg_scales, w1, w2, gate, offs, pos1, pos2, pos3, pos4):
    wg = unpack_weight(wg_words, wg_scales, "e2m1")
    w1q = mxq(f64(w1), 1, "e4m3")
    w2q = mxq(f64(w2), 1, "e4m3")
    idx = unstriped(offs)
    x = unpack_weight(x_words, x_scales, "e4m3")
    o = sigmoid(wg.T @ x)
    h = relu(by_expert(w1q, x[:, idx]))
    y = by_expert(w2q, mxq(h, 0, "e4m3"))
    c = sum(f64(gate[r, :1]) * y[:, unstriped(p)] for r, p in enumerate((pos1, pos2, pos3, pos4)))
    out_0 = o * c
    return (out_0,) + planes(out_0)

@@ -1,0 +1,264 @@
+from contextlib import ExitStack
+
+import concourse.mybir as mybir
+from concourse.masks import make_identity
+
+K, T, E, C, H, N, TOP = 512, 512, 8, 256, 512, 512, 4
+SLOTS = E * C
+FLOPS = 2 * (K * N * T + SLOTS * (K * H + H * N))
+
+F32 = mybir.dt.float32
+BF16 = mybir.dt.bfloat16
+I32 = mybir.dt.int32
+U32 = mybir.dt.uint32
+U16 = mybir.dt.uint16
+U8 = mybir.dt.uint8
+FP8X4 = mybir.dt.float8_e4m3fn_x4
+FP4X4 = mybir.dt.float4_e2m1fn_x4
+ACT = mybir.ActivationFunctionType
+MULT = mybir.AluOpType.mult
+
+P = 128
+PACK = 4
+BLOCKS = N // P
+PAIRS = E // 2
+HALF = N // 2
+SCALAR_CASTS = 2
+
+
+def tile_moe_ogt_relu_sigmoid_kernel(
+    tc, x_words, x_scales, wg_words, wg_scales, w1, w2, gate, offs, pos1, pos2, pos3, pos4, out_0, out_1, out_2
+):
+    nc = tc.nc
+    with ExitStack() as ctx:
+        keep = ctx.enter_context(tc.tile_pool(name="keep", bufs=1))
+        ring = ctx.enter_context(tc.tile_pool(name="ring", bufs=1))
+        psum = ctx.enter_context(tc.psum_pool(name="psum", bufs=1))
+
+        def load_scale_rows(plane, rows):
+            nc.vector.memset(plane[:].bitcast(I32), 0)
+            for r in range(4):
+                nc.sync.dma_start(out=plane[:].bitcast(I32)[r:P:32, :], in_=rows[0, r:16:4, :].bitcast(I32))
+
+        slot_list = keep.tile([P, SLOTS // 16], U16, name="slot_list")
+        nc.sync.dma_start(slot_list[:], offs)
+        xw = keep.tile([P, T], I32, name="xw", align_bytes=64)
+        nc.sync.dma_start(out=xw[:], in_=x_words[0].rearrange("p t d -> p (t d)").bitcast(I32))
+        xs = keep.tile([P, T], U8, name="xs", align_bytes=64)
+        load_scale_rows(xs, x_scales)
+
+        raw1 = {}
+        raw2 = {}
+
+        def load_w1(e):
+            raw1[e] = ring.tile([P, PACK, H], F32, name="raw1", bufs=4)
+            nc.sync.dma_start(out=raw1[e][:], in_=w1[e].rearrange("(p j) c -> p j c", j=PACK))
+
+        def load_w2(e, half):
+            raw2[e, half] = keep.tile([P, PACK, HALF], F32, name="raw2_%d_%d" % (e, half))
+            cols = slice(half * HALF, (half + 1) * HALF)
+            nc.sync.dma_start(out=raw2[e, half][:], in_=w2[e].rearrange("(p j) c -> p j c", j=PACK)[:, :, cols])
+
+        load_w1(0)
+        load_w1(1)
+        gw = keep.tile([P, 2 * N], U8, name="gw", align_bytes=64)
+        nc.sync.dma_start(out=gw[:].bitcast(I32), in_=wg_words[0].bitcast(I32))
+        gs = keep.tile([P, N], U8, name="gs", align_bytes=64)
+        load_scale_rows(gs, wg_scales)
+        load_w1(2)
+        load_w1(3)
+        back_lists = []
+        for r, pos in enumerate((pos1, pos2, pos3, pos4)):
+            lst = keep.tile([P, T // 16], U16, name="back_list%d" % r)
+            nc.sync.dma_start(lst[:], pos)
+            back_lists.append(lst)
+
+        ident = keep.tile([P, P], F32, name="ident")
+        make_identity(nc, ident[:])
+
+        xg, xgs, hq, hs = {}, {}, {}, {}
+
+        def gather_tokens(e):
+            offsets = slot_list[:, e * C // 16 : (e + 1) * C // 16]
+            xg[e] = keep.tile([P, C], U32, name="xg%d" % e, align_bytes=64)
+            xgs[e] = keep.tile([P, C], U8, name="xgs%d" % e, align_bytes=64)
+            nc.vector.tensor_copy(xg[e][:], xw[:].bitcast(U32).indirect(offsets))
+            nc.vector.tensor_copy(xgs[e][:], xs[:].indirect(offsets))
+
+        w1b, w1q, w1s, hb = {}, {}, {}, {}
+
+        def cast_w1(e):
+            w1b[e] = ring.tile([P, PACK * H], BF16, name="w1b", bufs=2, align_bytes=64)
+            dst = w1b[e][:].rearrange("p (t m j) -> p m t j", t=PACK, j=PACK)
+            src = raw1[e][:].rearrange("p j (m t) -> p m t j", t=PACK)
+            if e < SCALAR_CASTS:
+                nc.scalar.copy(out=dst, in_=src)
+            else:
+                nc.vector.tensor_copy(out=dst, in_=src)
+
+        def quantize_w1(e):
+            w1q[e] = ring.tile([P, H], U32, name="w1q", bufs=2, align_bytes=64)
+            w1s[e] = ring.tile([P, H], U8, name="w1s", bufs=2, align_bytes=64)
+            nc.vector.quantize_mx(out=w1q[e][:].bitcast(FP8X4), scales=w1s[e][:], in_=w1b[e][:])
+
+        def first_layer(e):
+            hb[e] = ring.tile([P, C, PACK], BF16, name="hb", bufs=2, align_bytes=64)
+            for s in range(C // P):
+                slots = slice(s * P, (s + 1) * P)
+                bank = psum.tile([P, PACK, P], F32, name="wide_bank", bufs=4)
+                for t in range(PACK):
+                    cols = slice(t * P, (t + 1) * P)
+                    nc.tensor.matmul_mx(
+                        out=bank[:, t, :],
+                        lhsT=w1q[e][:, cols].bitcast(FP8X4),
+                        lhsT_scale=w1s[e][:, cols],
+                        rhs=xg[e][:, slots].bitcast(FP8X4),
+                        rhs_scale=xgs[e][:, slots],
+                        start=True,
+                        stop=True,
+                    )
+                nc.scalar.activation(out=hb[e][:, slots, :], in_=bank[:].rearrange("p t s -> p s t"), func=ACT.Relu)
+
+        def quantize_h(e):
+            hq[e] = keep.tile([P, C], U32, name="hq%d" % e, align_bytes=64)
+            hs[e] = keep.tile([P, C], U8, name="hs%d" % e, align_bytes=64)
+            nc.vector.quantize_mx(
+                out=hq[e][:].bitcast(FP8X4), scales=hs[e][:], in_=hb[e][:].rearrange("p s t -> p (s t)")
+            )
+
+        og = {}
+
+        def output_gate(b):
+            bank = psum.tile([P, T // P, P], F32, name="wide_bank", bufs=4)
+            for c in range(T // P):
+                toks = slice(c * P, (c + 1) * P)
+                nc.tensor.matmul_mx(
+                    out=bank[:, c, :],
+                    lhsT=xw[:, toks].bitcast(FP8X4),
+                    lhsT_scale=xs[:, toks],
+                    rhs=gw[:, 2 * b * P : 2 * (b + 1) * P].bitcast(FP4X4),
+                    rhs_scale=gs[:, b * P : (b + 1) * P],
+                    start=True,
+                    stop=True,
+                )
+            og[b] = keep.tile([P, T // P, PACK, P // PACK], F32, name="og%d" % b)
+            nc.scalar.activation(
+                out=og[b][:], in_=bank[:].rearrange("p c (q t) -> p c t q", t=PACK), func=ACT.Sigmoid
+            )
+
+        y = {}
+
+        def second_layer(b, pair):
+            if pair == 0:
+                y[b] = ring.tile([P, SLOTS], F32, name="y", bufs=2)
+            w2b = ring.tile([P, 2, P, PACK], BF16, name="shared%d" % pair, bufs=1, align_bytes=64)
+            first = (b % 2) * P
+            for u in range(2):
+                src = raw2[2 * pair + u, b // 2][:, :, first : first + P]
+                nc.scalar.copy(
+                    out=w2b[:, u, :, :].rearrange("p (c i) j -> p c j i", i=4),
+                    in_=src.rearrange("p j (c i) -> p c j i", i=4),
+                )
+            w2q = ring.tile([P, 2 * P], U32, name="w2q", bufs=2, align_bytes=64)
+            w2s = ring.tile([P, 2 * P], U8, name="w2s", bufs=2, align_bytes=64)
+            nc.vector.quantize_mx(
+                out=w2q[:].bitcast(FP8X4), scales=w2s[:], in_=w2b[:].rearrange("p u c j -> p (u c j)")
+            )
+            bank = psum.tile([P, 2 * C], F32, name="y_bank", bufs=2)
+            for u in range(2):
+                e = 2 * pair + u
+                nc.tensor.matmul_mx(
+                    out=bank[:, u * C : (u + 1) * C],
+                    lhsT=w2q[:, u * P : (u + 1) * P].bitcast(FP8X4),
+                    lhsT_scale=w2s[:, u * P : (u + 1) * P],
+                    rhs=hq[e][:].bitcast(FP8X4),
+                    rhs_scale=hs[e][:],
+                    start=True,
+                    stop=True,
+                )
+            nc.scalar.copy(out=y[b][:, 2 * C * pair : 2 * C * (pair + 1)], in_=bank[:])
+
+        gather_tokens(0)
+        gather_tokens(1)
+        for step in range(E + 2):
+            if step < E:
+                cast_w1(step)
+                if step + 4 < E:
+                    load_w1(step + 4)
+            if step + 2 < E:
+                gather_tokens(step + 2)
+            if step >= 2:
+                quantize_h(step - 2)
+            if step < E:
+                quantize_w1(step)
+            if 1 <= step <= E:
+                first_layer(step - 1)
+            if step == 1:
+                for b in range(BLOCKS):
+                    output_gate(b)
+
+        for e in range(E):
+            load_w2(e, 0)
+        gates = []
+        for r in range(TOP):
+            g = keep.tile([P, T], F32, name="gate%d" % r)
+            nc.sync.dma_start(out=g[:], in_=gate[r])
+            gates.append(g)
+        for e in range(E):
+            load_w2(e, 1)
+
+        for pair in range(PAIRS):
+            second_layer(0, pair)
+
+        gated = keep.tile([P, T // P, PACK, P], F32, name="gated")
+        for b in range(BLOCKS):
+            total = psum.tile([P, T // P, P], F32, name="sum_bank", bufs=2)
+            for r in range(TOP):
+                if b + 1 < BLOCKS:
+                    second_layer(b + 1, r)
+                picked = ring.tile([P, T], F32, name="shared%d" % r, bufs=1, align_bytes=64)
+                nc.vector.tensor_tensor(picked[:], y[b][:].indirect(back_lists[r][:]), gates[r][:], MULT)
+                for c in range(T // P):
+                    nc.tensor.matmul(
+                        total[:, c, :],
+                        picked[:, c * P : (c + 1) * P],
+                        ident[:],
+                        start=(r == 0 and c == 0),
+                        stop=(r == TOP - 1 and c == T // P - 1),
+                        is_transpose=True,
+                    )
+            q0 = b * P // PACK
+            nc.vector.tensor_tensor(
+                gated[:, :, :, q0 : q0 + P // PACK],
+                total[:].rearrange("p c (q t) -> p c t q", t=PACK),
+                og[b][:],
+                MULT,
+            )
+
+        result = keep.tile([P, PACK, T], F32, name="result")
+        rounded = keep.tile([P, T, PACK], BF16, name="rounded", align_bytes=64)
+        codes = keep.tile([P, T], I32, name="codes", align_bytes=64)
+        scales = keep.tile([P, T], U8, name="scales", align_bytes=64)
+        out_rows = out_0.rearrange("(p t) k -> p t k", t=PACK)
+        out_words = out_1[0].rearrange("p k d -> p (k d)").bitcast(I32)
+        for c in range(T // P):
+            toks = slice(c * P, (c + 1) * P)
+            bank = psum.tile([P, PACK, P], F32, name="wide_bank", bufs=4)
+            for t in range(PACK):
+                nc.tensor.transpose(bank[:, t, :], gated[:, c, t, :], ident[:])
+            nc.scalar.copy(out=result[:, :, toks], in_=bank[:])
+            nc.vector.tensor_copy(out=rounded[:, toks, :], in_=result[:, :, toks].rearrange("p t k -> p k t"))
+            if c % 2 == 1:
+                both = slice((c - 1) * P, (c + 1) * P)
+                nc.sync.dma_start(out=out_rows[:, :, both], in_=result[:, :, both])
+                nc.vector.quantize_mx(
+                    out=codes[:, both].bitcast(FP8X4),
+                    scales=scales[:, both],
+                    in_=rounded[:, both, :].rearrange("p k t -> p (k t)"),
+                )
+                nc.sync.dma_start(out=out_words[:, both], in_=codes[:, both])
+        for quad in range(4):
+            nc.sync.dma_start(
+                out=out_2[0, 4 * quad : 4 * quad + 4, :].bitcast(I32),
+                in_=scales[:].bitcast(I32)[32 * quad : 32 * quad + 4, :],
+            )

@@ -23,7 +23,15 @@ PACK = 4
 BLOCKS = N // P
 PAIRS = E // 2
 HALF = N // 2
-SCALAR_CASTS = 2
+WINDOW = 704
+HOLD = 0
+GPOS = 0
+STAGES = 7
+VCAST = (0, 0, 1, 1, 0)
+LEAD = 4
+PER = 1
+CUTS = (0, 0, 0, 64, 64, 128, 128, 128)
+LAST_CHUNKS = ((0, 2), (2, 3), (3, 4))
 
 
 def tile_moe_ogt_relu_sigmoid_kernel(
@@ -36,38 +44,44 @@ def tile_moe_ogt_relu_sigmoid_kernel(
         psum = ctx.enter_context(tc.psum_pool(name="psum", bufs=1))
 
         def load_scale_rows(plane, rows):
-            nc.vector.memset(plane[:].bitcast(I32), 0)
+            nc.gpsimd.memset(plane[:].bitcast(I32), 0)
             for r in range(4):
-                nc.sync.dma_start(out=plane[:].bitcast(I32)[r:P:32, :], in_=rows[0, r:16:4, :].bitcast(I32))
+                nc.sync.dma_start(out=plane[:].bitcast(I32)[r:P:32, : T // 4], in_=rows[0, r:16:4, :].bitcast(I32))
+
+        def bank(index, shape):
+            return psum.tile(shape, F32, name="bank%d" % index, bufs=1)
 
         slot_list = keep.tile([P, SLOTS // 16], U16, name="slot_list")
         nc.sync.dma_start(slot_list[:], offs)
-        xw = keep.tile([P, T], I32, name="xw", align_bytes=64)
-        nc.sync.dma_start(out=xw[:], in_=x_words[0].rearrange("p t d -> p (t d)").bitcast(I32))
-        xs = keep.tile([P, T], U8, name="xs", align_bytes=64)
+        xw = keep.tile([P, WINDOW], I32, name="xw", align_bytes=64)
+        nc.gpsimd.memset(xw[:, T:], 0)
+        nc.sync.dma_start(out=xw[:, :T], in_=x_words[0].rearrange("p t d -> p (t d)").bitcast(I32))
+        xs = keep.tile([P, WINDOW], U8, name="xs", align_bytes=64)
         load_scale_rows(xs, x_scales)
 
-        raw1 = {}
-        raw2 = {}
+        raw1, raw2, back_lists, gates = {}, {}, [], []
 
-        def load_w1(e):
-            raw1[e] = ring.tile([P, PACK, H], F32, name="raw1", bufs=4)
-            nc.sync.dma_start(out=raw1[e][:], in_=w1[e].rearrange("(p j) c -> p j c", j=PACK))
+        def load_w1(e, pieces=1):
+            raw1[e] = ring.tile([P, PACK, H], F32, name="raw%d" % e, bufs=1)
+            for i in range(pieces):
+                rows = slice(i * PACK // pieces, (i + 1) * PACK // pieces)
+                nc.sync.dma_start(out=raw1[e][:, rows, :], in_=w1[e].rearrange("(p j) c -> p j c", j=PACK)[:, rows, :])
 
         def load_w2(e, half):
-            raw2[e, half] = keep.tile([P, PACK, HALF], F32, name="raw2_%d_%d" % (e, half))
+            raw2[e, half] = ring.tile([P, PACK, HALF], F32, name="raw%d" % (e + E * (1 - half)), bufs=1)
             cols = slice(half * HALF, (half + 1) * HALF)
             nc.sync.dma_start(out=raw2[e, half][:], in_=w2[e].rearrange("(p j) c -> p j c", j=PACK)[:, :, cols])
 
-        load_w1(0)
-        load_w1(1)
-        gw = keep.tile([P, 2 * N], U8, name="gw", align_bytes=64)
-        nc.sync.dma_start(out=gw[:].bitcast(I32), in_=wg_words[0].bitcast(I32))
-        gs = keep.tile([P, N], U8, name="gs", align_bytes=64)
-        load_scale_rows(gs, wg_scales)
-        load_w1(2)
-        load_w1(3)
-        back_lists = []
+        load_w1(0, 2)
+        pending = list(range(E))
+        for e in range(1, E):
+            load_w1(e)
+            if e >= LEAD:
+                for u in range(PER):
+                    if pending:
+                        load_w2(pending.pop(0), 0)
+        for e in pending:
+            load_w2(e, 0)
         for r, pos in enumerate((pos1, pos2, pos3, pos4)):
             lst = keep.tile([P, T // 16], U16, name="back_list%d" % r)
             nc.sync.dma_start(lst[:], pos)
@@ -75,26 +89,32 @@ def tile_moe_ogt_relu_sigmoid_kernel(
 
         ident = keep.tile([P, P], F32, name="ident")
         make_identity(nc, ident[:])
+        warm = keep.tile([P, 1], F32, name="warm")
+        nc.scalar.activation(out=warm[:], in_=ident[:, 0:1], func=ACT.Sigmoid)
 
         xg, xgs, hq, hs = {}, {}, {}, {}
 
-        def gather_tokens(e):
-            offsets = slot_list[:, e * C // 16 : (e + 1) * C // 16]
-            xg[e] = keep.tile([P, C], U32, name="xg%d" % e, align_bytes=64)
-            xgs[e] = keep.tile([P, C], U8, name="xgs%d" % e, align_bytes=64)
-            nc.vector.tensor_copy(xg[e][:], xw[:].bitcast(U32).indirect(offsets))
-            nc.vector.tensor_copy(xgs[e][:], xs[:].indirect(offsets))
+        def gather_words(pair, tag):
+            xg[pair] = ring.tile([P, 2 * C], U32, name=tag, bufs=1, align_bytes=64)
+            offsets = slot_list[:, pair * C // 8 : (pair + 1) * C // 8]
+            nc.vector.tensor_copy(xg[pair][:], xw[:].bitcast(U32).indirect(offsets))
+
+        def gather_scales(pair, tag):
+            xgs[pair] = ring.tile([P, 2 * C], U8, name=tag, bufs=1, align_bytes=64)
+            offsets = slot_list[:, pair * C // 8 : (pair + 1) * C // 8]
+            nc.vector.tensor_copy(xgs[pair][:], xs[:].indirect(offsets))
 
         w1b, w1q, w1s, hb = {}, {}, {}, {}
 
         def cast_w1(e):
-            w1b[e] = ring.tile([P, PACK * H], BF16, name="w1b", bufs=2, align_bytes=64)
+            w1b[e] = ring.tile([P, PACK * H], BF16, name="w1b%d" % (e % STAGES), bufs=1, align_bytes=64)
             dst = w1b[e][:].rearrange("p (t m j) -> p m t j", t=PACK, j=PACK)
             src = raw1[e][:].rearrange("p j (m t) -> p m t j", t=PACK)
-            if e < SCALAR_CASTS:
-                nc.scalar.copy(out=dst, in_=src)
-            else:
-                nc.vector.tensor_copy(out=dst, in_=src)
+            cut = CUTS[e]
+            if cut > 0:
+                nc.vector.tensor_copy(out=dst[:, :cut, :, :], in_=src[:, :cut, :, :])
+            if cut < P:
+                nc.scalar.copy(out=dst[:, cut:, :, :], in_=src[:, cut:, :, :])
 
         def quantize_w1(e):
             w1q[e] = ring.tile([P, H], U32, name="w1q", bufs=2, align_bytes=64)
@@ -102,22 +122,23 @@ def tile_moe_ogt_relu_sigmoid_kernel(
             nc.vector.quantize_mx(out=w1q[e][:].bitcast(FP8X4), scales=w1s[e][:], in_=w1b[e][:])
 
         def first_layer(e):
-            hb[e] = ring.tile([P, C, PACK], BF16, name="hb", bufs=2, align_bytes=64)
+            hb[e] = ring.tile([P, C, PACK], BF16, name="hb", bufs=3, align_bytes=64)
             for s in range(C // P):
                 slots = slice(s * P, (s + 1) * P)
-                bank = psum.tile([P, PACK, P], F32, name="wide_bank", bufs=4)
+                picked = slice((e % 2) * C + s * P, (e % 2) * C + (s + 1) * P)
+                sums = bank(4 + (2 * e + s) % 4, [P, PACK, P])
                 for t in range(PACK):
                     cols = slice(t * P, (t + 1) * P)
                     nc.tensor.matmul_mx(
-                        out=bank[:, t, :],
+                        out=sums[:, t, :],
                         lhsT=w1q[e][:, cols].bitcast(FP8X4),
                         lhsT_scale=w1s[e][:, cols],
-                        rhs=xg[e][:, slots].bitcast(FP8X4),
-                        rhs_scale=xgs[e][:, slots],
+                        rhs=xg[e // 2][:, picked].bitcast(FP8X4),
+                        rhs_scale=xgs[e // 2][:, picked],
                         start=True,
                         stop=True,
                     )
-                nc.scalar.activation(out=hb[e][:, slots, :], in_=bank[:].rearrange("p t s -> p s t"), func=ACT.Relu)
+                nc.scalar.activation(out=hb[e][:, slots, :], in_=sums[:].rearrange("p t s -> p s t"), func=ACT.Relu)
 
         def quantize_h(e):
             hq[e] = keep.tile([P, C], U32, name="hq%d" % e, align_bytes=64)
@@ -128,12 +149,12 @@ def tile_moe_ogt_relu_sigmoid_kernel(
 
         og = {}
 
-        def output_gate(b):
-            bank = psum.tile([P, T // P, P], F32, name="wide_bank", bufs=4)
+        def output_gate(b, index):
+            sums = bank(index, [P, T // P, P])
             for c in range(T // P):
                 toks = slice(c * P, (c + 1) * P)
                 nc.tensor.matmul_mx(
-                    out=bank[:, c, :],
+                    out=sums[:, c, :],
                     lhsT=xw[:, toks].bitcast(FP8X4),
                     lhsT_scale=xs[:, toks],
                     rhs=gw[:, 2 * b * P : 2 * (b + 1) * P].bitcast(FP4X4),
@@ -143,32 +164,34 @@ def tile_moe_ogt_relu_sigmoid_kernel(
                 )
             og[b] = keep.tile([P, T // P, PACK, P // PACK], F32, name="og%d" % b)
             nc.scalar.activation(
-                out=og[b][:], in_=bank[:].rearrange("p c (q t) -> p c t q", t=PACK), func=ACT.Sigmoid
+                out=og[b][:], in_=sums[:].rearrange("p c (q t) -> p c t q", t=PACK), func=ACT.Sigmoid
             )
 
-        y = {}
+        y, w2b, y_sums = {}, {}, {}
 
-        def second_layer(b, pair):
-            if pair == 0:
-                y[b] = ring.tile([P, SLOTS], F32, name="y", bufs=2)
-            w2b = ring.tile([P, 2, P, PACK], BF16, name="shared%d" % pair, bufs=1, align_bytes=64)
+        def cast_w2(b, e0, count, tag, on_vector=False):
+            w2b[b, e0] = ring.tile([P, count, P, PACK], BF16, name=tag, bufs=1, align_bytes=64)
+            copy = nc.vector.tensor_copy if on_vector else nc.scalar.copy
             first = (b % 2) * P
-            for u in range(2):
-                src = raw2[2 * pair + u, b // 2][:, :, first : first + P]
-                nc.scalar.copy(
-                    out=w2b[:, u, :, :].rearrange("p (c i) j -> p c j i", i=4),
+            for u in range(count):
+                src = raw2[e0 + u, b // 2][:, :, first : first + P]
+                copy(
+                    out=w2b[b, e0][:, u, :, :].rearrange("p (c i) j -> p c j i", i=4),
                     in_=src.rearrange("p j (c i) -> p c j i", i=4),
                 )
-            w2q = ring.tile([P, 2 * P], U32, name="w2q", bufs=2, align_bytes=64)
-            w2s = ring.tile([P, 2 * P], U8, name="w2s", bufs=2, align_bytes=64)
+
+        def second_layer(b, e0, count, tag):
+            w2q = ring.tile([P, count * P], U32, name=tag, bufs=1, align_bytes=64)
+            w2s = ring.tile([P, count * P], U8, name="w2s", bufs=2, align_bytes=64)
             nc.vector.quantize_mx(
-                out=w2q[:].bitcast(FP8X4), scales=w2s[:], in_=w2b[:].rearrange("p u c j -> p (u c j)")
+                out=w2q[:].bitcast(FP8X4), scales=w2s[:], in_=w2b[b, e0][:].rearrange("p u c j -> p (u c j)")
             )
-            bank = psum.tile([P, 2 * C], F32, name="y_bank", bufs=2)
-            for u in range(2):
-                e = 2 * pair + u
+            for u in range(count):
+                e = e0 + u
+                if u % 2 == 0:
+                    y_sums[b, e // 2] = bank(e // 2, [P, 2 * C])
                 nc.tensor.matmul_mx(
-                    out=bank[:, u * C : (u + 1) * C],
+                    out=y_sums[b, e // 2][:, (u % 2) * C : (u % 2 + 1) * C],
                     lhsT=w2q[:, u * P : (u + 1) * P].bitcast(FP8X4),
                     lhsT_scale=w2s[:, u * P : (u + 1) * P],
                     rhs=hq[e][:].bitcast(FP8X4),
@@ -176,64 +199,92 @@ def tile_moe_ogt_relu_sigmoid_kernel(
                     start=True,
                     stop=True,
                 )
-            nc.scalar.copy(out=y[b][:, 2 * C * pair : 2 * C * (pair + 1)], in_=bank[:])
 
-        gather_tokens(0)
-        gather_tokens(1)
+        def keep_y(b, e0, count):
+            if e0 == 0:
+                y[b] = ring.tile([P, SLOTS], F32, name="y", bufs=2)
+            for pair in range(e0 // 2, (e0 + count) // 2):
+                nc.scalar.copy(out=y[b][:, 2 * C * pair : 2 * C * (pair + 1)], in_=y_sums[b, pair][:])
+
+        def pick(b, r, toks, tag, total, first_chunk):
+            width = toks.stop - toks.start
+            picked = ring.tile([P, width], F32, name=tag, bufs=1, align_bytes=64)
+            offsets = back_lists[r][:, toks.start // 16 : toks.stop // 16]
+            nc.vector.tensor_tensor(picked[:], y[b][:].indirect(offsets), gates[r][:, toks], MULT)
+            for c in range(width // P):
+                nc.tensor.matmul(
+                    total[:, c, :],
+                    picked[:, c * P : (c + 1) * P],
+                    ident[:],
+                    start=(r == 0 and c == 0),
+                    stop=(r == TOP - 1 and c == width // P - 1),
+                    is_transpose=True,
+                )
+
+        def apply_gate(b, chunks, total):
+            q0 = b * P // PACK
+            nc.vector.tensor_tensor(
+                gated[:, chunks, :, q0 : q0 + P // PACK],
+                total[:].rearrange("p c (q t) -> p c t q", t=PACK),
+                og[b][:, chunks, :, :],
+                MULT,
+            )
+
+        for pair in range(2):
+            gather_words(pair, "xg%d" % pair)
+            gather_scales(pair, "xgs%d" % pair)
         for step in range(E + 2):
             if step < E:
                 cast_w1(step)
-                if step + 4 < E:
-                    load_w1(step + 4)
-            if step + 2 < E:
-                gather_tokens(step + 2)
             if step >= 2:
                 quantize_h(step - 2)
             if step < E:
                 quantize_w1(step)
+                if 0 <= step - HOLD < 4:
+                    late = (gather_words, gather_scales)[(step - HOLD) % 2]
+                    late(2 + (step - HOLD) // 2, "w1b%d" % step)
             if 1 <= step <= E:
                 first_layer(step - 1)
-            if step == 1:
-                for b in range(BLOCKS):
-                    output_gate(b)
 
-        for e in range(E):
-            load_w2(e, 0)
-        gates = []
+        gw = keep.tile([P, 2 * N], U8, name="gw", align_bytes=64)
+        gs = keep.tile([P, N], U8, name="gs", align_bytes=64)
         for r in range(TOP):
+            if r == GPOS:
+                nc.sync.dma_start(out=gw[:].bitcast(I32), in_=wg_words[0].bitcast(I32))
+                load_scale_rows(gs, wg_scales)
             g = keep.tile([P, T], F32, name="gate%d" % r)
             nc.sync.dma_start(out=g[:], in_=gate[r])
             gates.append(g)
-        for e in range(E):
+            load_w2(r, 1)
+        for e in range(TOP, E):
             load_w2(e, 1)
 
+        cast_w2(0, 0, 2, "pair0", VCAST[0])
         for pair in range(PAIRS):
-            second_layer(0, pair)
+            if pair + 1 < PAIRS:
+                if pair + 2 == PAIRS:
+                    cast_w2(1, 0, 4, "slot0", VCAST[4])
+                cast_w2(0, 2 * pair + 2, 2, "pair%d" % ((pair + 1) % 2), VCAST[pair + 1])
+            second_layer(0, 2 * pair, 2, "codes%d" % (pair % 2))
+            keep_y(0, 2 * pair, 2)
+        cast_w2(1, 4, 4, "slot2")
 
         gated = keep.tile([P, T // P, PACK, P], F32, name="gated")
-        for b in range(BLOCKS):
-            total = psum.tile([P, T // P, P], F32, name="sum_bank", bufs=2)
-            for r in range(TOP):
-                if b + 1 < BLOCKS:
-                    second_layer(b + 1, r)
-                picked = ring.tile([P, T], F32, name="shared%d" % r, bufs=1, align_bytes=64)
-                nc.vector.tensor_tensor(picked[:], y[b][:].indirect(back_lists[r][:]), gates[r][:], MULT)
-                for c in range(T // P):
-                    nc.tensor.matmul(
-                        total[:, c, :],
-                        picked[:, c * P : (c + 1) * P],
-                        ident[:],
-                        start=(r == 0 and c == 0),
-                        stop=(r == TOP - 1 and c == T // P - 1),
-                        is_transpose=True,
-                    )
-            q0 = b * P // PACK
-            nc.vector.tensor_tensor(
-                gated[:, :, :, q0 : q0 + P // PACK],
-                total[:].rearrange("p c (q t) -> p c t q", t=PACK),
-                og[b][:],
-                MULT,
-            )
+        everyone = slice(0, T)
+        totals = {}
+        for b in range(BLOCKS - 1):
+            totals[b] = bank(4 + b % 2, [P, T // P, P])
+            for half in range(2):
+                second_layer(b + 1, 4 * half, 4, "slot%d" % (2 * half + 1))
+                pick(b, 2 * half, everyone, "slot%d" % (2 * half), totals[b], 0)
+                if half == 0 and b > 0:
+                    apply_gate(b - 1, slice(0, T // P), totals[b - 1])
+                pick(b, 2 * half + 1, everyone, "slot%d" % (2 * half + 1), totals[b], 0)
+                keep_y(b + 1, 4 * half, 4)
+                if b + 2 < BLOCKS:
+                    cast_w2(b + 2, 4 * half, 4, "slot%d" % (2 * half))
+            output_gate(b, 3)
+        output_gate(BLOCKS - 1, 2)
 
         result = keep.tile([P, PACK, T], F32, name="result")
         rounded = keep.tile([P, T, PACK], BF16, name="rounded", align_bytes=64)
@@ -241,22 +292,32 @@ def tile_moe_ogt_relu_sigmoid_kernel(
         scales = keep.tile([P, T], U8, name="scales", align_bytes=64)
         out_rows = out_0.rearrange("(p t) k -> p t k", t=PACK)
         out_words = out_1[0].rearrange("p k d -> p (k d)").bitcast(I32)
-        for c in range(T // P):
-            toks = slice(c * P, (c + 1) * P)
-            bank = psum.tile([P, PACK, P], F32, name="wide_bank", bufs=4)
-            for t in range(PACK):
-                nc.tensor.transpose(bank[:, t, :], gated[:, c, t, :], ident[:])
-            nc.scalar.copy(out=result[:, :, toks], in_=bank[:])
-            nc.vector.tensor_copy(out=rounded[:, toks, :], in_=result[:, :, toks].rearrange("p t k -> p k t"))
-            if c % 2 == 1:
-                both = slice((c - 1) * P, (c + 1) * P)
-                nc.sync.dma_start(out=out_rows[:, :, both], in_=result[:, :, both])
-                nc.vector.quantize_mx(
-                    out=codes[:, both].bitcast(FP8X4),
-                    scales=scales[:, both],
-                    in_=rounded[:, both, :].rearrange("p k t -> p (k t)"),
-                )
-                nc.sync.dma_start(out=out_words[:, both], in_=codes[:, both])
+        last = BLOCKS - 1
+        for i, (c0, c1) in enumerate(LAST_CHUNKS):
+            toks = slice(c0 * P, c1 * P)
+            total = bank(5 + i, [P, c1 - c0, P])
+            for r in range(TOP):
+                pick(last, r, toks, "slot%d" % r, total, c0)
+                if i == 0 and r == 0:
+                    apply_gate(last - 1, slice(0, T // P), totals[last - 1])
+            apply_gate(last, slice(c0, c1), total)
+            for c in range(c0, c1):
+                chunk = slice(c * P, (c + 1) * P)
+                turned = bank(c, [P, PACK, P])
+                for t in range(PACK):
+                    nc.tensor.transpose(turned[:, t, :], gated[:, c, t, :], ident[:])
+                if i + 1 < len(LAST_CHUNKS):
+                    nc.scalar.copy(out=rounded[:, chunk, :], in_=turned[:].rearrange("p t k -> p k t"))
+                else:
+                    nc.vector.tensor_copy(out=rounded[:, chunk, :], in_=turned[:].rearrange("p t k -> p k t"))
+                nc.scalar.copy(out=result[:, :, chunk], in_=turned[:])
+            nc.sync.dma_start(out=out_rows[:, :, toks], in_=result[:, :, toks])
+            nc.vector.quantize_mx(
+                out=codes[:, toks].bitcast(FP8X4),
+                scales=scales[:, toks],
+                in_=rounded[:, toks, :].rearrange("p k t -> p (k t)"),
+            )
+            nc.sync.dma_start(out=out_words[:, toks], in_=codes[:, toks])
         for quad in range(4):
             nc.sync.dma_start(
                 out=out_2[0, 4 * quad : 4 * quad + 4, :].bitcast(I32),

@@ -25,12 +25,15 @@ PAIRS = E // 2
 HALF = N // 2
 WINDOW = 704
 HOLD = 0
-GPOS = 0
+GPOS = 7
+PERCHUNK = 1
+WORDS_AT = (2, 3, 4)
+GATE_AT = 4
+STAGE_TAGS = ("pair0", "pair1", "pair0", "pair1")
 STAGES = 7
-VCAST = (0, 0, 1, 1, 0)
-LEAD = 4
-PER = 1
-CUTS = (0, 0, 0, 64, 64, 128, 128, 128)
+VCAST = (0, 0, 0, 1, 1)
+LEAD = 3
+CUTS = (0, 0, 64, 64, 64, 64, 128, 128)
 LAST_CHUNKS = ((0, 2), (2, 3), (3, 4))
 
 
@@ -54,38 +57,53 @@ def tile_moe_ogt_relu_sigmoid_kernel(
         slot_list = keep.tile([P, SLOTS // 16], U16, name="slot_list")
         nc.sync.dma_start(slot_list[:], offs)
         xw = keep.tile([P, WINDOW], I32, name="xw", align_bytes=64)
-        nc.gpsimd.memset(xw[:, T:], 0)
         nc.sync.dma_start(out=xw[:, :T], in_=x_words[0].rearrange("p t d -> p (t d)").bitcast(I32))
         xs = keep.tile([P, WINDOW], U8, name="xs", align_bytes=64)
         load_scale_rows(xs, x_scales)
+        nc.gpsimd.memset(xw[:, T:], 0)
 
         raw1, raw2, back_lists, gates = {}, {}, [], []
 
-        def load_w1(e, pieces=1):
-            raw1[e] = ring.tile([P, PACK, H], F32, name="raw%d" % e, bufs=1)
+        def load_w1(e):
+            rows = w1[e].rearrange("(p j) c -> p j c", j=PACK)
+            pieces = 2 if e == 0 else 1
+            raw1[e] = []
             for i in range(pieces):
-                rows = slice(i * PACK // pieces, (i + 1) * PACK // pieces)
-                nc.sync.dma_start(out=raw1[e][:, rows, :], in_=w1[e].rearrange("(p j) c -> p j c", j=PACK)[:, rows, :])
+                piece = ring.tile([P, PACK, H // pieces], F32, name="raw%d" % (e + 2 * E * i), bufs=1)
+                nc.sync.dma_start(out=piece[:], in_=rows[:, :, i * H // pieces : (i + 1) * H // pieces])
+                raw1[e].append(piece)
 
-        def load_w2(e, half):
-            raw2[e, half] = ring.tile([P, PACK, HALF], F32, name="raw%d" % (e + E * (1 - half)), bufs=1)
-            cols = slice(half * HALF, (half + 1) * HALF)
-            nc.sync.dma_start(out=raw2[e, half][:], in_=w2[e].rearrange("(p j) c -> p j c", j=PACK)[:, :, cols])
+        def load_w2(e, b):
+            tag = ("first%d", "second%d", "raw%d", "first%d")[b] % e
+            raw2[e, b] = ring.tile([P, PACK, P], F32, name=tag, bufs=1)
+            cols = slice(b * P, (b + 1) * P)
+            nc.sync.dma_start(out=raw2[e, b][:], in_=w2[e].rearrange("(p j) c -> p j c", j=PACK)[:, :, cols])
 
-        load_w1(0, 2)
-        pending = list(range(E))
+        def load_gate(r):
+            g = keep.tile([P, T], F32, name="gate%d" % r)
+            nc.sync.dma_start(out=g[:], in_=gate[r])
+            gates.append(g)
+
+        gw = keep.tile([P, 2 * N], U8, name="gw", align_bytes=64)
+        gs = keep.tile([P, N], U8, name="gs", align_bytes=64)
+        load_w1(0)
         for e in range(1, E):
             load_w1(e)
+            if e <= TOP:
+                lst = keep.tile([P, T // 16], U16, name="back_list%d" % e)
+                nc.sync.dma_start(lst[:], (pos1, pos2, pos3, pos4)[e - 1])
+                back_lists.append(lst)
             if e >= LEAD:
-                for u in range(PER):
-                    if pending:
-                        load_w2(pending.pop(0), 0)
-        for e in pending:
+                load_w2(e - LEAD, 0)
+            if e == GPOS:
+                load_scale_rows(gs, wg_scales)
+                nc.sync.dma_start(out=gw[:].bitcast(I32), in_=wg_words[0].bitcast(I32))
+        for e in range(E - LEAD, E):
             load_w2(e, 0)
-        for r, pos in enumerate((pos1, pos2, pos3, pos4)):
-            lst = keep.tile([P, T // 16], U16, name="back_list%d" % r)
-            nc.sync.dma_start(lst[:], pos)
-            back_lists.append(lst)
+        for e in range(E):
+            load_w2(e, 1)
+            if e >= GATE_AT and len(gates) < TOP:
+                load_gate(len(gates))
 
         ident = keep.tile([P, P], F32, name="ident")
         make_identity(nc, ident[:])
@@ -108,13 +126,16 @@ def tile_moe_ogt_relu_sigmoid_kernel(
 
         def cast_w1(e):
             w1b[e] = ring.tile([P, PACK * H], BF16, name="w1b%d" % (e % STAGES), bufs=1, align_bytes=64)
-            dst = w1b[e][:].rearrange("p (t m j) -> p m t j", t=PACK, j=PACK)
-            src = raw1[e][:].rearrange("p j (m t) -> p m t j", t=PACK)
-            cut = CUTS[e]
-            if cut > 0:
-                nc.vector.tensor_copy(out=dst[:, :cut, :, :], in_=src[:, :cut, :, :])
-            if cut < P:
-                nc.scalar.copy(out=dst[:, cut:, :, :], in_=src[:, cut:, :, :])
+            dst = w1b[e][:].rearrange("p (u v m j) -> p m u j v", u=2, v=2, j=PACK)
+            width = P // len(raw1[e])
+            for i, piece in enumerate(raw1[e]):
+                src = piece[:].rearrange("p j (m u v) -> p m u j v", u=2, v=2)
+                part = dst[:, i * width : (i + 1) * width]
+                cut = CUTS[e] * width // P
+                if cut > 0:
+                    nc.vector.tensor_copy(out=part[:, :cut], in_=src[:, :cut])
+                if cut < width:
+                    nc.scalar.copy(out=part[:, cut:], in_=src[:, cut:])
 
         def quantize_w1(e):
             w1q[e] = ring.tile([P, H], U32, name="w1q", bufs=2, align_bytes=64)
@@ -149,7 +170,7 @@ def tile_moe_ogt_relu_sigmoid_kernel(
 
         og = {}
 
-        def output_gate(b, index):
+        def output_gate(b, index, tag):
             sums = bank(index, [P, T // P, P])
             for c in range(T // P):
                 toks = slice(c * P, (c + 1) * P)
@@ -162,7 +183,7 @@ def tile_moe_ogt_relu_sigmoid_kernel(
                     start=True,
                     stop=True,
                 )
-            og[b] = keep.tile([P, T // P, PACK, P // PACK], F32, name="og%d" % b)
+            og[b] = ring.tile([P, T // P, PACK, P // PACK], F32, name=tag, bufs=1, align_bytes=64)
             nc.scalar.activation(
                 out=og[b][:], in_=sums[:].rearrange("p c (q t) -> p c t q", t=PACK), func=ACT.Sigmoid
             )
@@ -172,9 +193,8 @@ def tile_moe_ogt_relu_sigmoid_kernel(
         def cast_w2(b, e0, count, tag, on_vector=False):
             w2b[b, e0] = ring.tile([P, count, P, PACK], BF16, name=tag, bufs=1, align_bytes=64)
             copy = nc.vector.tensor_copy if on_vector else nc.scalar.copy
-            first = (b % 2) * P
             for u in range(count):
-                src = raw2[e0 + u, b // 2][:, :, first : first + P]
+                src = raw2[e0 + u, b][:]
                 copy(
                     out=w2b[b, e0][:, u, :, :].rearrange("p (c i) j -> p c j i", i=4),
                     in_=src.rearrange("p j (c i) -> p c j i", i=4),
@@ -182,7 +202,10 @@ def tile_moe_ogt_relu_sigmoid_kernel(
 
         def second_layer(b, e0, count, tag):
             w2q = ring.tile([P, count * P], U32, name=tag, bufs=1, align_bytes=64)
-            w2s = ring.tile([P, count * P], U8, name="w2s", bufs=2, align_bytes=64)
+            if b >= 2 and e0 == 0:
+                w2s = ring.tile([P, count * P], U8, name="held%d" % b, bufs=1, align_bytes=64)
+            else:
+                w2s = ring.tile([P, count * P], U8, name="w2s", bufs=2, align_bytes=64)
             nc.vector.quantize_mx(
                 out=w2q[:].bitcast(FP8X4), scales=w2s[:], in_=w2b[b, e0][:].rearrange("p u c j -> p (u c j)")
             )
@@ -246,28 +269,20 @@ def tile_moe_ogt_relu_sigmoid_kernel(
             if 1 <= step <= E:
                 first_layer(step - 1)
 
-        gw = keep.tile([P, 2 * N], U8, name="gw", align_bytes=64)
-        gs = keep.tile([P, N], U8, name="gs", align_bytes=64)
-        for r in range(TOP):
-            if r == GPOS:
-                nc.sync.dma_start(out=gw[:].bitcast(I32), in_=wg_words[0].bitcast(I32))
-                load_scale_rows(gs, wg_scales)
-            g = keep.tile([P, T], F32, name="gate%d" % r)
-            nc.sync.dma_start(out=g[:], in_=gate[r])
-            gates.append(g)
-            load_w2(r, 1)
-        for e in range(TOP, E):
-            load_w2(e, 1)
+        for e in range(E):
+            load_w2(e, 2)
 
         cast_w2(0, 0, 2, "pair0", VCAST[0])
         for pair in range(PAIRS):
             if pair + 1 < PAIRS:
                 if pair + 2 == PAIRS:
                     cast_w2(1, 0, 4, "slot0", VCAST[4])
-                cast_w2(0, 2 * pair + 2, 2, "pair%d" % ((pair + 1) % 2), VCAST[pair + 1])
+                cast_w2(0, 2 * pair + 2, 2, STAGE_TAGS[pair + 1], VCAST[pair + 1])
             second_layer(0, 2 * pair, 2, "codes%d" % (pair % 2))
             keep_y(0, 2 * pair, 2)
         cast_w2(1, 4, 4, "slot2")
+        for e in range(E):
+            load_w2(e, 3)
 
         gated = keep.tile([P, T // P, PACK, P], F32, name="gated")
         everyone = slice(0, T)
@@ -277,14 +292,15 @@ def tile_moe_ogt_relu_sigmoid_kernel(
             for half in range(2):
                 second_layer(b + 1, 4 * half, 4, "slot%d" % (2 * half + 1))
                 pick(b, 2 * half, everyone, "slot%d" % (2 * half), totals[b], 0)
-                if half == 0 and b > 0:
-                    apply_gate(b - 1, slice(0, T // P), totals[b - 1])
                 pick(b, 2 * half + 1, everyone, "slot%d" % (2 * half + 1), totals[b], 0)
                 keep_y(b + 1, 4 * half, 4)
+                if half == 0 and b > 0:
+                    output_gate(b - 1, 6 + b % 2, "held%d" % (b + 1))
+                    apply_gate(b - 1, slice(0, T // P), totals[b - 1])
                 if b + 2 < BLOCKS:
                     cast_w2(b + 2, 4 * half, 4, "slot%d" % (2 * half))
-            output_gate(b, 3)
-        output_gate(BLOCKS - 1, 2)
+        output_gate(BLOCKS - 2, 3, "og2")
+        output_gate(BLOCKS - 1, 2, "og3")
 
         result = keep.tile([P, PACK, T], F32, name="result")
         rounded = keep.tile([P, T, PACK], BF16, name="rounded", align_bytes=64)
@@ -295,7 +311,7 @@ def tile_moe_ogt_relu_sigmoid_kernel(
         last = BLOCKS - 1
         for i, (c0, c1) in enumerate(LAST_CHUNKS):
             toks = slice(c0 * P, c1 * P)
-            total = bank(5 + i, [P, c1 - c0, P])
+            total = bank((6, 7, 5)[i], [P, c1 - c0, P])
             for r in range(TOP):
                 pick(last, r, toks, "slot%d" % r, total, c0)
                 if i == 0 and r == 0:
@@ -306,18 +322,27 @@ def tile_moe_ogt_relu_sigmoid_kernel(
                 turned = bank(c, [P, PACK, P])
                 for t in range(PACK):
                     nc.tensor.transpose(turned[:, t, :], gated[:, c, t, :], ident[:])
-                if i + 1 < len(LAST_CHUNKS):
+                if c + 1 < T // P:
+                    nc.scalar.copy(out=result[:, :, chunk], in_=turned[:])
                     nc.scalar.copy(out=rounded[:, chunk, :], in_=turned[:].rearrange("p t k -> p k t"))
                 else:
                     nc.vector.tensor_copy(out=rounded[:, chunk, :], in_=turned[:].rearrange("p t k -> p k t"))
-                nc.scalar.copy(out=result[:, :, chunk], in_=turned[:])
-            nc.sync.dma_start(out=out_rows[:, :, toks], in_=result[:, :, toks])
+                    turned = bank(0, [P, PACK, P])
+                    for t in range(PACK):
+                        nc.tensor.transpose(turned[:, t, :], gated[:, c, t, :], ident[:])
+                    nc.scalar.copy(out=result[:, :, chunk], in_=turned[:])
+                if PERCHUNK:
+                    nc.sync.dma_start(out=out_rows[:, :, chunk], in_=result[:, :, chunk])
+            if not PERCHUNK:
+                nc.sync.dma_start(out=out_rows[:, :, toks], in_=result[:, :, toks])
             nc.vector.quantize_mx(
                 out=codes[:, toks].bitcast(FP8X4),
                 scales=scales[:, toks],
                 in_=rounded[:, toks, :].rearrange("p k t -> p (k t)"),
             )
-            nc.sync.dma_start(out=out_words[:, toks], in_=codes[:, toks])
+            if c1 in WORDS_AT:
+                done = slice(max([0] + [w for w in WORDS_AT if w < c1]) * P, c1 * P)
+                nc.sync.dma_start(out=out_words[:, done], in_=codes[:, done])
         for quad in range(4):
             nc.sync.dma_start(
                 out=out_2[0, 4 * quad : 4 * quad + 4, :].bitcast(I32),

@@ -20,21 +20,24 @@ MULT = mybir.AluOpType.mult
 
 P = 128
 PACK = 4
+STRIPE = 16
 BLOCKS = N // P
-PAIRS = E // 2
-HALF = N // 2
+CHUNKS = T // P
+UNIT = E // 2
 WINDOW = 704
-HOLD = 0
-GPOS = 7
-PERCHUNK = 1
-WORDS_AT = (2, 3, 4)
-GATE_AT = 4
-STAGE_TAGS = ("pair0", "pair1", "pair0", "pair1")
-STAGES = 7
-VCAST = (0, 0, 0, 1, 1)
-LEAD = 3
-CUTS = (0, 0, 64, 64, 64, 64, 128, 128)
-LAST_CHUNKS = ((0, 2), (2, 3), (3, 4))
+
+VECTOR_SHARE_EARLY, VECTOR_SHARE_LATE = 64, 96
+LAST_RANGES = ((0, 2), (2, 3), (3, 4))
+
+ROOM = PACK * H * 4
+QUARTER = ROOM // 4
+W2_FIRST = E * ROOM
+W2_SECOND = W2_FIRST + E * QUARTER
+EARLY_TOKENS = W2_SECOND + E * QUARTER
+
+
+def w2_place(e, b):
+    return (W2_FIRST + e * QUARTER, W2_SECOND + e * QUARTER, e * ROOM + 2 * QUARTER, W2_FIRST + e * QUARTER)[b]
 
 
 def tile_moe_ogt_relu_sigmoid_kernel(
@@ -44,17 +47,24 @@ def tile_moe_ogt_relu_sigmoid_kernel(
     with ExitStack() as ctx:
         keep = ctx.enter_context(tc.tile_pool(name="keep", bufs=1))
         ring = ctx.enter_context(tc.tile_pool(name="ring", bufs=1))
+        placed = ctx.enter_context(tc.tile_pool(name="placed", bufs=1))
         psum = ctx.enter_context(tc.psum_pool(name="psum", bufs=1))
+
+        def place(shape, dtype, name, offset):
+            return placed.tile(shape, dtype, name=name, offset=offset, align_bytes=64)
+
+        def tenant(shape, dtype, tag):
+            return ring.tile(shape, dtype, name=tag, bufs=1, align_bytes=64)
+
+        def bank(index, shape):
+            return psum.tile(shape, F32, name="bank%d" % index, bufs=1)
 
         def load_scale_rows(plane, rows):
             nc.gpsimd.memset(plane[:].bitcast(I32), 0)
             for r in range(4):
                 nc.sync.dma_start(out=plane[:].bitcast(I32)[r:P:32, : T // 4], in_=rows[0, r:16:4, :].bitcast(I32))
 
-        def bank(index, shape):
-            return psum.tile(shape, F32, name="bank%d" % index, bufs=1)
-
-        slot_list = keep.tile([P, SLOTS // 16], U16, name="slot_list")
+        slot_list = keep.tile([P, SLOTS // STRIPE], U16, name="slot_list")
         nc.sync.dma_start(slot_list[:], offs)
         xw = keep.tile([P, WINDOW], I32, name="xw", align_bytes=64)
         nc.sync.dma_start(out=xw[:, :T], in_=x_words[0].rearrange("p t d -> p (t d)").bitcast(I32))
@@ -69,73 +79,64 @@ def tile_moe_ogt_relu_sigmoid_kernel(
             pieces = 2 if e == 0 else 1
             raw1[e] = []
             for i in range(pieces):
-                piece = ring.tile([P, PACK, H // pieces], F32, name="raw%d" % (e + 2 * E * i), bufs=1)
+                piece = place([P, PACK, H // pieces], F32, "raw1_%d_%d" % (e, i), e * ROOM + i * ROOM // 2)
                 nc.sync.dma_start(out=piece[:], in_=rows[:, :, i * H // pieces : (i + 1) * H // pieces])
                 raw1[e].append(piece)
 
         def load_w2(e, b):
-            tag = ("first%d", "second%d", "raw%d", "first%d")[b] % e
-            raw2[e, b] = ring.tile([P, PACK, P], F32, name=tag, bufs=1)
-            cols = slice(b * P, (b + 1) * P)
-            nc.sync.dma_start(out=raw2[e, b][:], in_=w2[e].rearrange("(p j) c -> p j c", j=PACK)[:, :, cols])
+            raw2[e, b] = place([P, PACK, P], F32, "raw2_%d_%d" % (e, b), w2_place(e, b))
+            rows = w2[e].rearrange("(p j) c -> p j c", j=PACK)
+            nc.sync.dma_start(out=raw2[e, b][:], in_=rows[:, :, b * P : (b + 1) * P])
 
-        def load_gate(r):
-            g = keep.tile([P, T], F32, name="gate%d" % r)
-            nc.sync.dma_start(out=g[:], in_=gate[r])
-            gates.append(g)
-
-        gw = keep.tile([P, 2 * N], U8, name="gw", align_bytes=64)
-        gs = keep.tile([P, N], U8, name="gs", align_bytes=64)
+        wg_codes = keep.tile([P, 2 * N], U8, name="wg_codes", align_bytes=64)
+        wg_plane = keep.tile([P, N], U8, name="wg_plane", align_bytes=64)
         load_w1(0)
         for e in range(1, E):
             load_w1(e)
             if e <= TOP:
-                lst = keep.tile([P, T // 16], U16, name="back_list%d" % e)
-                nc.sync.dma_start(lst[:], (pos1, pos2, pos3, pos4)[e - 1])
-                back_lists.append(lst)
-            if e >= LEAD:
-                load_w2(e - LEAD, 0)
-            if e == GPOS:
-                load_scale_rows(gs, wg_scales)
-                nc.sync.dma_start(out=gw[:].bitcast(I32), in_=wg_words[0].bitcast(I32))
-        for e in range(E - LEAD, E):
-            load_w2(e, 0)
+                back_list = keep.tile([P, T // STRIPE], U16, name="back_list%d" % e)
+                nc.sync.dma_start(back_list[:], (pos1, pos2, pos3, pos4)[e - 1])
+                back_lists.append(back_list)
+            load_w2(e - 1, 0)
+        load_scale_rows(wg_plane, wg_scales)
+        nc.sync.dma_start(out=wg_codes[:].bitcast(I32), in_=wg_words[0].bitcast(I32))
+        load_w2(E - 1, 0)
         for e in range(E):
             load_w2(e, 1)
-            if e >= GATE_AT and len(gates) < TOP:
-                load_gate(len(gates))
+            if e >= UNIT:
+                gate_row = keep.tile([P, T], F32, name="gate%d" % (e - UNIT))
+                nc.sync.dma_start(out=gate_row[:], in_=gate[e - UNIT])
+                gates.append(gate_row)
 
         ident = keep.tile([P, P], F32, name="ident")
         make_identity(nc, ident[:])
         warm = keep.tile([P, 1], F32, name="warm")
         nc.scalar.activation(out=warm[:], in_=ident[:, 0:1], func=ACT.Sigmoid)
 
-        xg, xgs, hq, hs = {}, {}, {}, {}
+        xg, xgs, w1b, w1q, w1s, hb, hq, hs = {}, {}, {}, {}, {}, {}, {}, {}
 
-        def gather_words(pair, tag):
-            xg[pair] = ring.tile([P, 2 * C], U32, name=tag, bufs=1, align_bytes=64)
-            offsets = slot_list[:, pair * C // 8 : (pair + 1) * C // 8]
-            nc.vector.tensor_copy(xg[pair][:], xw[:].bitcast(U32).indirect(offsets))
+        def pair_offsets(pair):
+            return slot_list[:, 2 * pair * C // STRIPE : 2 * (pair + 1) * C // STRIPE]
 
-        def gather_scales(pair, tag):
-            xgs[pair] = ring.tile([P, 2 * C], U8, name=tag, bufs=1, align_bytes=64)
-            offsets = slot_list[:, pair * C // 8 : (pair + 1) * C // 8]
-            nc.vector.tensor_copy(xgs[pair][:], xs[:].indirect(offsets))
+        def gather_words(pair, offset):
+            xg[pair] = place([P, 2 * C], U32, "xg%d" % pair, offset)
+            nc.vector.tensor_copy(xg[pair][:], xw[:].bitcast(U32).indirect(pair_offsets(pair)))
 
-        w1b, w1q, w1s, hb = {}, {}, {}, {}
+        def gather_scales(pair, offset):
+            xgs[pair] = place([P, 2 * C], U8, "xgs%d" % pair, offset)
+            nc.vector.tensor_copy(xgs[pair][:], xs[:].indirect(pair_offsets(pair)))
 
         def cast_w1(e):
-            w1b[e] = ring.tile([P, PACK * H], BF16, name="w1b%d" % (e % STAGES), bufs=1, align_bytes=64)
+            w1b[e] = ring.tile([P, PACK * H], BF16, name="w1b", bufs=3, align_bytes=64)
             dst = w1b[e][:].rearrange("p (u v m j) -> p m u j v", u=2, v=2, j=PACK)
             width = P // len(raw1[e])
+            cut = 0 if e == 0 else VECTOR_SHARE_EARLY if e < UNIT else VECTOR_SHARE_LATE
             for i, piece in enumerate(raw1[e]):
                 src = piece[:].rearrange("p j (m u v) -> p m u j v", u=2, v=2)
                 part = dst[:, i * width : (i + 1) * width]
-                cut = CUTS[e] * width // P
                 if cut > 0:
                     nc.vector.tensor_copy(out=part[:, :cut], in_=src[:, :cut])
-                if cut < width:
-                    nc.scalar.copy(out=part[:, cut:], in_=src[:, cut:])
+                nc.scalar.copy(out=part[:, cut:], in_=src[:, cut:])
 
         def quantize_w1(e):
             w1q[e] = ring.tile([P, H], U32, name="w1q", bufs=2, align_bytes=64)
@@ -143,10 +144,10 @@ def tile_moe_ogt_relu_sigmoid_kernel(
             nc.vector.quantize_mx(out=w1q[e][:].bitcast(FP8X4), scales=w1s[e][:], in_=w1b[e][:])
 
         def first_layer(e):
-            hb[e] = ring.tile([P, C, PACK], BF16, name="hb", bufs=3, align_bytes=64)
+            hb[e] = place([P, C, PACK], BF16, "hb%d" % e, (e + 1) * ROOM if e + 1 < E else w2_place(e, 0))
             for s in range(C // P):
-                slots = slice(s * P, (s + 1) * P)
-                picked = slice((e % 2) * C + s * P, (e % 2) * C + (s + 1) * P)
+                own = slice(s * P, (s + 1) * P)
+                in_pair = slice((e % 2) * C + s * P, (e % 2) * C + (s + 1) * P)
                 sums = bank(4 + (2 * e + s) % 4, [P, PACK, P])
                 for t in range(PACK):
                     cols = slice(t * P, (t + 1) * P)
@@ -154,56 +155,56 @@ def tile_moe_ogt_relu_sigmoid_kernel(
                         out=sums[:, t, :],
                         lhsT=w1q[e][:, cols].bitcast(FP8X4),
                         lhsT_scale=w1s[e][:, cols],
-                        rhs=xg[e // 2][:, picked].bitcast(FP8X4),
-                        rhs_scale=xgs[e // 2][:, picked],
+                        rhs=xg[e // 2][:, in_pair].bitcast(FP8X4),
+                        rhs_scale=xgs[e // 2][:, in_pair],
                         start=True,
                         stop=True,
                     )
-                nc.scalar.activation(out=hb[e][:, slots, :], in_=sums[:].rearrange("p t s -> p s t"), func=ACT.Relu)
+                nc.scalar.activation(out=hb[e][:, own, :], in_=sums[:].rearrange("p t s -> p s t"), func=ACT.Relu)
 
         def quantize_h(e):
-            hq[e] = keep.tile([P, C], U32, name="hq%d" % e, align_bytes=64)
+            offset = (e + 2) % E * ROOM + QUARTER if e + 1 < E else w2_place(UNIT - 1, 1)
+            hq[e] = place([P, C], U32, "hq%d" % e, offset)
             hs[e] = keep.tile([P, C], U8, name="hs%d" % e, align_bytes=64)
             nc.vector.quantize_mx(
                 out=hq[e][:].bitcast(FP8X4), scales=hs[e][:], in_=hb[e][:].rearrange("p s t -> p (s t)")
             )
 
-        og = {}
+        og, y, w2b, y_sums = {}, {}, {}, {}
 
         def output_gate(b, index, tag):
-            sums = bank(index, [P, T // P, P])
-            for c in range(T // P):
+            sums = bank(index, [P, CHUNKS, P])
+            for c in range(CHUNKS):
                 toks = slice(c * P, (c + 1) * P)
                 nc.tensor.matmul_mx(
                     out=sums[:, c, :],
                     lhsT=xw[:, toks].bitcast(FP8X4),
                     lhsT_scale=xs[:, toks],
-                    rhs=gw[:, 2 * b * P : 2 * (b + 1) * P].bitcast(FP4X4),
-                    rhs_scale=gs[:, b * P : (b + 1) * P],
+                    rhs=wg_codes[:, 2 * b * P : 2 * (b + 1) * P].bitcast(FP4X4),
+                    rhs_scale=wg_plane[:, b * P : (b + 1) * P],
                     start=True,
                     stop=True,
                 )
-            og[b] = ring.tile([P, T // P, PACK, P // PACK], F32, name=tag, bufs=1, align_bytes=64)
+            og[b] = tenant([P, CHUNKS, PACK, P // PACK], F32, tag)
             nc.scalar.activation(
                 out=og[b][:], in_=sums[:].rearrange("p c (q t) -> p c t q", t=PACK), func=ACT.Sigmoid
             )
 
-        y, w2b, y_sums = {}, {}, {}
-
-        def cast_w2(b, e0, count, tag, on_vector=False):
-            w2b[b, e0] = ring.tile([P, count, P, PACK], BF16, name=tag, bufs=1, align_bytes=64)
-            copy = nc.vector.tensor_copy if on_vector else nc.scalar.copy
-            for u in range(count):
-                src = raw2[e0 + u, b][:]
+        def cast_w2(b, e0, count, tag, members, copy):
+            if members[0] == 0:
+                w2b[b, e0] = tenant([P, count, P, PACK], BF16, tag)
+            for u in members:
                 copy(
                     out=w2b[b, e0][:, u, :, :].rearrange("p (c i) j -> p c j i", i=4),
-                    in_=src.rearrange("p j (c i) -> p c j i", i=4),
+                    in_=raw2[e0 + u, b][:].rearrange("p j (c i) -> p c j i", i=4),
                 )
 
         def second_layer(b, e0, count, tag):
-            w2q = ring.tile([P, count * P], U32, name=tag, bufs=1, align_bytes=64)
+            w2q = tenant([P, count * P], U32, tag)
             if b >= 2 and e0 == 0:
-                w2s = ring.tile([P, count * P], U8, name="held%d" % b, bufs=1, align_bytes=64)
+                w2s = tenant([P, count * P], U8, "before_og%d" % (b - 2))
+            elif b == 1 and e0 == 0:
+                w2s = place([P, count * P], U8, "w2s_behind_h", w2_place(E - 1, 0))
             else:
                 w2s = ring.tile([P, count * P], U8, name="w2s", bufs=2, align_bytes=64)
             nc.vector.quantize_mx(
@@ -224,15 +225,21 @@ def tile_moe_ogt_relu_sigmoid_kernel(
                 )
 
         def keep_y(b, e0, count):
-            if e0 == 0:
+            if e0 == 0 and b == 1:
+                y[b] = place([P, SLOTS], F32, "y1", w2_place(UNIT, 1))
+            elif e0 == 0:
                 y[b] = ring.tile([P, SLOTS], F32, name="y", bufs=2)
             for pair in range(e0 // 2, (e0 + count) // 2):
                 nc.scalar.copy(out=y[b][:, 2 * C * pair : 2 * C * (pair + 1)], in_=y_sums[b, pair][:])
 
-        def pick(b, r, toks, tag, total, first_chunk):
+        def pick(b, r, toks, total):
             width = toks.stop - toks.start
-            picked = ring.tile([P, width], F32, name=tag, bufs=1, align_bytes=64)
-            offsets = back_lists[r][:, toks.start // 16 : toks.stop // 16]
+            if 0 < b < BLOCKS - 1 and r % 2 == 0:
+                last_of_unit = UNIT * (r // 2) + UNIT - 1
+                picked = place([P, width], F32, "picked%d_%d" % (b, r), w2_place(last_of_unit, b + 1))
+            else:
+                picked = tenant([P, width], F32, "slot%d" % r)
+            offsets = back_lists[r][:, toks.start // STRIPE : toks.stop // STRIPE]
             nc.vector.tensor_tensor(picked[:], y[b][:].indirect(offsets), gates[r][:, toks], MULT)
             for c in range(width // P):
                 nc.tensor.matmul(
@@ -245,60 +252,58 @@ def tile_moe_ogt_relu_sigmoid_kernel(
                 )
 
         def apply_gate(b, chunks, total):
-            q0 = b * P // PACK
+            p0 = b * P // PACK
             nc.vector.tensor_tensor(
-                gated[:, chunks, :, q0 : q0 + P // PACK],
+                gated[:, chunks, :, p0 : p0 + P // PACK],
                 total[:].rearrange("p c (q t) -> p c t q", t=PACK),
                 og[b][:, chunks, :, :],
                 MULT,
             )
 
         for pair in range(2):
-            gather_words(pair, "xg%d" % pair)
-            gather_scales(pair, "xgs%d" % pair)
+            gather_words(pair, EARLY_TOKENS + 2 * pair * QUARTER)
+            gather_scales(pair, EARLY_TOKENS + (2 * pair + 1) * QUARTER)
         for step in range(E + 2):
             if step < E:
                 cast_w1(step)
+            else:
+                cast_w2(1, 0, UNIT, "slot0", (2 * (step - E), 2 * (step - E) + 1), nc.vector.tensor_copy)
             if step >= 2:
                 quantize_h(step - 2)
             if step < E:
                 quantize_w1(step)
-                if 0 <= step - HOLD < 4:
-                    late = (gather_words, gather_scales)[(step - HOLD) % 2]
-                    late(2 + (step - HOLD) // 2, "w1b%d" % step)
+            if 1 <= step <= UNIT:
+                gather = gather_words if step % 2 == 1 else gather_scales
+                gather(2 + (step - 1) // 2, step * ROOM + 3 * QUARTER)
             if 1 <= step <= E:
-                first_layer(step - 1)
+                e = step - 1
+                cast_w2(0, e - e % 2, 2, "pair%d" % (e // 2 % 2), (e % 2,), nc.scalar.copy)
+                first_layer(e)
+            if step >= 3 and step % 2 == 1:
+                second_layer(0, step - 3, 2, "codes%d" % ((step - 3) // 2 % 2))
+                keep_y(0, step - 3, 2)
 
         for e in range(E):
             load_w2(e, 2)
+        cast_w2(1, UNIT, UNIT, "slot2", range(UNIT), nc.scalar.copy)
 
-        cast_w2(0, 0, 2, "pair0", VCAST[0])
-        for pair in range(PAIRS):
-            if pair + 1 < PAIRS:
-                if pair + 2 == PAIRS:
-                    cast_w2(1, 0, 4, "slot0", VCAST[4])
-                cast_w2(0, 2 * pair + 2, 2, STAGE_TAGS[pair + 1], VCAST[pair + 1])
-            second_layer(0, 2 * pair, 2, "codes%d" % (pair % 2))
-            keep_y(0, 2 * pair, 2)
-        cast_w2(1, 4, 4, "slot2")
-        for e in range(E):
-            load_w2(e, 3)
-
-        gated = keep.tile([P, T // P, PACK, P], F32, name="gated")
-        everyone = slice(0, T)
+        gated = keep.tile([P, CHUNKS, PACK, P], F32, name="gated")
         totals = {}
         for b in range(BLOCKS - 1):
-            totals[b] = bank(4 + b % 2, [P, T // P, P])
+            totals[b] = bank(4 + b % 2, [P, CHUNKS, P])
             for half in range(2):
-                second_layer(b + 1, 4 * half, 4, "slot%d" % (2 * half + 1))
-                pick(b, 2 * half, everyone, "slot%d" % (2 * half), totals[b], 0)
-                pick(b, 2 * half + 1, everyone, "slot%d" % (2 * half + 1), totals[b], 0)
-                keep_y(b + 1, 4 * half, 4)
+                second_layer(b + 1, UNIT * half, UNIT, "slot%d" % (2 * half + 1))
+                if b == 0 and half == 0:
+                    for e in range(E):
+                        load_w2(e, 3)
+                pick(b, 2 * half, slice(0, T), totals[b])
+                pick(b, 2 * half + 1, slice(0, T), totals[b])
+                keep_y(b + 1, UNIT * half, UNIT)
                 if half == 0 and b > 0:
-                    output_gate(b - 1, 6 + b % 2, "held%d" % (b + 1))
-                    apply_gate(b - 1, slice(0, T // P), totals[b - 1])
+                    output_gate(b - 1, 6 + b % 2, "before_og%d" % (b - 1))
+                    apply_gate(b - 1, slice(0, CHUNKS), totals[b - 1])
                 if b + 2 < BLOCKS:
-                    cast_w2(b + 2, 4 * half, 4, "slot%d" % (2 * half))
+                    cast_w2(b + 2, UNIT * half, UNIT, "slot%d" % (2 * half), range(UNIT), nc.scalar.copy)
         output_gate(BLOCKS - 2, 3, "og2")
         output_gate(BLOCKS - 1, 2, "og3")
 
@@ -308,41 +313,38 @@ def tile_moe_ogt_relu_sigmoid_kernel(
         scales = keep.tile([P, T], U8, name="scales", align_bytes=64)
         out_rows = out_0.rearrange("(p t) k -> p t k", t=PACK)
         out_words = out_1[0].rearrange("p k d -> p (k d)").bitcast(I32)
+
+        def turn_back(c, index):
+            turned = bank(index, [P, PACK, P])
+            for t in range(PACK):
+                nc.tensor.transpose(turned[:, t, :], gated[:, c, t, :], ident[:])
+            return turned
+
         last = BLOCKS - 1
-        for i, (c0, c1) in enumerate(LAST_CHUNKS):
+        for i, (c0, c1) in enumerate(LAST_RANGES):
             toks = slice(c0 * P, c1 * P)
             total = bank((6, 7, 5)[i], [P, c1 - c0, P])
             for r in range(TOP):
-                pick(last, r, toks, "slot%d" % r, total, c0)
+                pick(last, r, toks, total)
                 if i == 0 and r == 0:
-                    apply_gate(last - 1, slice(0, T // P), totals[last - 1])
+                    apply_gate(last - 1, slice(0, CHUNKS), totals[last - 1])
             apply_gate(last, slice(c0, c1), total)
             for c in range(c0, c1):
                 chunk = slice(c * P, (c + 1) * P)
-                turned = bank(c, [P, PACK, P])
-                for t in range(PACK):
-                    nc.tensor.transpose(turned[:, t, :], gated[:, c, t, :], ident[:])
-                if c + 1 < T // P:
+                turned = turn_back(c, c)
+                if c + 1 < CHUNKS:
                     nc.scalar.copy(out=result[:, :, chunk], in_=turned[:])
                     nc.scalar.copy(out=rounded[:, chunk, :], in_=turned[:].rearrange("p t k -> p k t"))
                 else:
                     nc.vector.tensor_copy(out=rounded[:, chunk, :], in_=turned[:].rearrange("p t k -> p k t"))
-                    turned = bank(0, [P, PACK, P])
-                    for t in range(PACK):
-                        nc.tensor.transpose(turned[:, t, :], gated[:, c, t, :], ident[:])
-                    nc.scalar.copy(out=result[:, :, chunk], in_=turned[:])
-                if PERCHUNK:
-                    nc.sync.dma_start(out=out_rows[:, :, chunk], in_=result[:, :, chunk])
-            if not PERCHUNK:
-                nc.sync.dma_start(out=out_rows[:, :, toks], in_=result[:, :, toks])
+                    nc.scalar.copy(out=result[:, :, chunk], in_=turn_back(c, 0)[:])
+                nc.sync.dma_start(out=out_rows[:, :, chunk], in_=result[:, :, chunk])
             nc.vector.quantize_mx(
                 out=codes[:, toks].bitcast(FP8X4),
                 scales=scales[:, toks],
                 in_=rounded[:, toks, :].rearrange("p k t -> p (k t)"),
             )
-            if c1 in WORDS_AT:
-                done = slice(max([0] + [w for w in WORDS_AT if w < c1]) * P, c1 * P)
-                nc.sync.dma_start(out=out_words[:, done], in_=codes[:, done])
+            nc.sync.dma_start(out=out_words[:, toks], in_=codes[:, toks])
         for quad in range(4):
             nc.sync.dma_start(
                 out=out_2[0, 4 * quad : 4 * quad + 4, :].bitcast(I32),

from contextlib import ExitStack

import concourse.mybir as mybir
from concourse.masks import make_identity

K, T, E, C, H, N, TOP = 512, 512, 8, 256, 512, 512, 4
SLOTS = E * C
FLOPS = 2 * (K * N * T + SLOTS * (K * H + H * N))

F32 = mybir.dt.float32
BF16 = mybir.dt.bfloat16
I32 = mybir.dt.int32
U32 = mybir.dt.uint32
U16 = mybir.dt.uint16
U8 = mybir.dt.uint8
FP8X4 = mybir.dt.float8_e4m3fn_x4
FP4X4 = mybir.dt.float4_e2m1fn_x4
ACT = mybir.ActivationFunctionType
MULT = mybir.AluOpType.mult

P = 128
PACK = 4
STRIPE = 16
BLOCKS = N // P
CHUNKS = T // P
UNIT = E // 2
WINDOW = 704

VECTOR_SHARE_EARLY, VECTOR_SHARE_LATE = 64, 96
LAST_RANGES = ((0, 2), (2, 3), (3, 4))

ROOM = PACK * H * 4
QUARTER = ROOM // 4
W2_FIRST = E * ROOM
W2_SECOND = W2_FIRST + E * QUARTER
EARLY_TOKENS = W2_SECOND + E * QUARTER


def w2_place(e, b):
    return (W2_FIRST + e * QUARTER, W2_SECOND + e * QUARTER, e * ROOM + 2 * QUARTER, W2_FIRST + e * QUARTER)[b]


def tile_moe_ogt_relu_sigmoid_kernel(
    tc, x_words, x_scales, wg_words, wg_scales, w1, w2, gate, offs, pos1, pos2, pos3, pos4, out_0, out_1, out_2
):
    nc = tc.nc
    with ExitStack() as ctx:
        keep = ctx.enter_context(tc.tile_pool(name="keep", bufs=1))
        ring = ctx.enter_context(tc.tile_pool(name="ring", bufs=1))
        placed = ctx.enter_context(tc.tile_pool(name="placed", bufs=1))
        psum = ctx.enter_context(tc.psum_pool(name="psum", bufs=1))

        def place(shape, dtype, name, offset):
            return placed.tile(shape, dtype, name=name, offset=offset, align_bytes=64)

        def tenant(shape, dtype, tag):
            return ring.tile(shape, dtype, name=tag, bufs=1, align_bytes=64)

        def bank(index, shape):
            return psum.tile(shape, F32, name="bank%d" % index, bufs=1)

        def load_scale_rows(plane, rows):
            nc.gpsimd.memset(plane[:].bitcast(I32), 0)
            for r in range(4):
                nc.sync.dma_start(out=plane[:].bitcast(I32)[r:P:32, : T // 4], in_=rows[0, r:16:4, :].bitcast(I32))

        slot_list = keep.tile([P, SLOTS // STRIPE], U16, name="slot_list")
        nc.sync.dma_start(slot_list[:], offs)
        xw = keep.tile([P, WINDOW], I32, name="xw", align_bytes=64)
        nc.sync.dma_start(out=xw[:, :T], in_=x_words[0].rearrange("p t d -> p (t d)").bitcast(I32))
        xs = keep.tile([P, WINDOW], U8, name="xs", align_bytes=64)
        load_scale_rows(xs, x_scales)
        nc.gpsimd.memset(xw[:, T:], 0)

        raw1, raw2, back_lists, gates = {}, {}, [], []

        def load_w1(e):
            rows = w1[e].rearrange("(p j) c -> p j c", j=PACK)
            pieces = 2 if e == 0 else 1
            raw1[e] = []
            for i in range(pieces):
                piece = place([P, PACK, H // pieces], F32, "raw1_%d_%d" % (e, i), e * ROOM + i * ROOM // 2)
                nc.sync.dma_start(out=piece[:], in_=rows[:, :, i * H // pieces : (i + 1) * H // pieces])
                raw1[e].append(piece)

        def load_w2(e, b):
            raw2[e, b] = place([P, PACK, P], F32, "raw2_%d_%d" % (e, b), w2_place(e, b))
            rows = w2[e].rearrange("(p j) c -> p j c", j=PACK)
            nc.sync.dma_start(out=raw2[e, b][:], in_=rows[:, :, b * P : (b + 1) * P])

        wg_codes = keep.tile([P, 2 * N], U8, name="wg_codes", align_bytes=64)
        wg_plane = keep.tile([P, N], U8, name="wg_plane", align_bytes=64)
        load_w1(0)
        for e in range(1, E):
            load_w1(e)
            if e <= TOP:
                back_list = keep.tile([P, T // STRIPE], U16, name="back_list%d" % e)
                nc.sync.dma_start(back_list[:], (pos1, pos2, pos3, pos4)[e - 1])
                back_lists.append(back_list)
            load_w2(e - 1, 0)
        load_scale_rows(wg_plane, wg_scales)
        nc.sync.dma_start(out=wg_codes[:].bitcast(I32), in_=wg_words[0].bitcast(I32))
        load_w2(E - 1, 0)
        for e in range(E):
            load_w2(e, 1)
            if e >= UNIT:
                gate_row = keep.tile([P, T], F32, name="gate%d" % (e - UNIT))
                nc.sync.dma_start(out=gate_row[:], in_=gate[e - UNIT])
                gates.append(gate_row)

        ident = keep.tile([P, P], F32, name="ident")
        make_identity(nc, ident[:])
        warm = keep.tile([P, 1], F32, name="warm")
        nc.scalar.activation(out=warm[:], in_=ident[:, 0:1], func=ACT.Sigmoid)

        xg, xgs, w1b, w1q, w1s, hb, hq, hs = {}, {}, {}, {}, {}, {}, {}, {}

        def pair_offsets(pair):
            return slot_list[:, 2 * pair * C // STRIPE : 2 * (pair + 1) * C // STRIPE]

        def gather_words(pair, offset):
            xg[pair] = place([P, 2 * C], U32, "xg%d" % pair, offset)
            nc.vector.tensor_copy(xg[pair][:], xw[:].bitcast(U32).indirect(pair_offsets(pair)))

        def gather_scales(pair, offset):
            xgs[pair] = place([P, 2 * C], U8, "xgs%d" % pair, offset)
            nc.vector.tensor_copy(xgs[pair][:], xs[:].indirect(pair_offsets(pair)))

        def cast_w1(e):
            w1b[e] = ring.tile([P, PACK * H], BF16, name="w1b", bufs=3, align_bytes=64)
            dst = w1b[e][:].rearrange("p (u v m j) -> p m u j v", u=2, v=2, j=PACK)
            width = P // len(raw1[e])
            cut = 0 if e == 0 else VECTOR_SHARE_EARLY if e < UNIT else VECTOR_SHARE_LATE
            for i, piece in enumerate(raw1[e]):
                src = piece[:].rearrange("p j (m u v) -> p m u j v", u=2, v=2)
                part = dst[:, i * width : (i + 1) * width]
                if cut > 0:
                    nc.vector.tensor_copy(out=part[:, :cut], in_=src[:, :cut])
                nc.scalar.copy(out=part[:, cut:], in_=src[:, cut:])

        def quantize_w1(e):
            w1q[e] = ring.tile([P, H], U32, name="w1q", bufs=2, align_bytes=64)
            w1s[e] = ring.tile([P, H], U8, name="w1s", bufs=2, align_bytes=64)
            nc.vector.quantize_mx(out=w1q[e][:].bitcast(FP8X4), scales=w1s[e][:], in_=w1b[e][:])

        def first_layer(e):
            hb[e] = place([P, C, PACK], BF16, "hb%d" % e, (e + 1) * ROOM if e + 1 < E else w2_place(e, 0))
            for s in range(C // P):
                own = slice(s * P, (s + 1) * P)
                in_pair = slice((e % 2) * C + s * P, (e % 2) * C + (s + 1) * P)
                sums = bank(4 + (2 * e + s) % 4, [P, PACK, P])
                for t in range(PACK):
                    cols = slice(t * P, (t + 1) * P)
                    nc.tensor.matmul_mx(
                        out=sums[:, t, :],
                        lhsT=w1q[e][:, cols].bitcast(FP8X4),
                        lhsT_scale=w1s[e][:, cols],
                        rhs=xg[e // 2][:, in_pair].bitcast(FP8X4),
                        rhs_scale=xgs[e // 2][:, in_pair],
                        start=True,
                        stop=True,
                    )
                nc.scalar.activation(out=hb[e][:, own, :], in_=sums[:].rearrange("p t s -> p s t"), func=ACT.Relu)

        def quantize_h(e):
            offset = (e + 2) % E * ROOM + QUARTER if e + 1 < E else w2_place(UNIT - 1, 1)
            hq[e] = place([P, C], U32, "hq%d" % e, offset)
            hs[e] = keep.tile([P, C], U8, name="hs%d" % e, align_bytes=64)
            nc.vector.quantize_mx(
                out=hq[e][:].bitcast(FP8X4), scales=hs[e][:], in_=hb[e][:].rearrange("p s t -> p (s t)")
            )

        og, y, w2b, y_sums = {}, {}, {}, {}

        def output_gate(b, index, tag):
            sums = bank(index, [P, CHUNKS, P])
            for c in range(CHUNKS):
                toks = slice(c * P, (c + 1) * P)
                nc.tensor.matmul_mx(
                    out=sums[:, c, :],
                    lhsT=xw[:, toks].bitcast(FP8X4),
                    lhsT_scale=xs[:, toks],
                    rhs=wg_codes[:, 2 * b * P : 2 * (b + 1) * P].bitcast(FP4X4),
                    rhs_scale=wg_plane[:, b * P : (b + 1) * P],
                    start=True,
                    stop=True,
                )
            og[b] = tenant([P, CHUNKS, PACK, P // PACK], F32, tag)
            nc.scalar.activation(
                out=og[b][:], in_=sums[:].rearrange("p c (q t) -> p c t q", t=PACK), func=ACT.Sigmoid
            )

        def cast_w2(b, e0, count, tag, members, copy):
            if members[0] == 0:
                w2b[b, e0] = tenant([P, count, P, PACK], BF16, tag)
            for u in members:
                copy(
                    out=w2b[b, e0][:, u, :, :].rearrange("p (c i) j -> p c j i", i=4),
                    in_=raw2[e0 + u, b][:].rearrange("p j (c i) -> p c j i", i=4),
                )

        def second_layer(b, e0, count, tag):
            w2q = tenant([P, count * P], U32, tag)
            if b >= 2 and e0 == 0:
                w2s = tenant([P, count * P], U8, "before_og%d" % (b - 2))
            elif b == 1 and e0 == 0:
                w2s = place([P, count * P], U8, "w2s_behind_h", w2_place(E - 1, 0))
            else:
                w2s = ring.tile([P, count * P], U8, name="w2s", bufs=2, align_bytes=64)
            nc.vector.quantize_mx(
                out=w2q[:].bitcast(FP8X4), scales=w2s[:], in_=w2b[b, e0][:].rearrange("p u c j -> p (u c j)")
            )
            for u in range(count):
                e = e0 + u
                if u % 2 == 0:
                    y_sums[b, e // 2] = bank(e // 2, [P, 2 * C])
                nc.tensor.matmul_mx(
                    out=y_sums[b, e // 2][:, (u % 2) * C : (u % 2 + 1) * C],
                    lhsT=w2q[:, u * P : (u + 1) * P].bitcast(FP8X4),
                    lhsT_scale=w2s[:, u * P : (u + 1) * P],
                    rhs=hq[e][:].bitcast(FP8X4),
                    rhs_scale=hs[e][:],
                    start=True,
                    stop=True,
                )

        def keep_y(b, e0, count):
            if e0 == 0 and b == 1:
                y[b] = place([P, SLOTS], F32, "y1", w2_place(UNIT, 1))
            elif e0 == 0:
                y[b] = ring.tile([P, SLOTS], F32, name="y", bufs=2)
            for pair in range(e0 // 2, (e0 + count) // 2):
                nc.scalar.copy(out=y[b][:, 2 * C * pair : 2 * C * (pair + 1)], in_=y_sums[b, pair][:])

        def pick(b, r, toks, total):
            width = toks.stop - toks.start
            if 0 < b < BLOCKS - 1 and r % 2 == 0:
                last_of_unit = UNIT * (r // 2) + UNIT - 1
                picked = place([P, width], F32, "picked%d_%d" % (b, r), w2_place(last_of_unit, b + 1))
            else:
                picked = tenant([P, width], F32, "slot%d" % r)
            offsets = back_lists[r][:, toks.start // STRIPE : toks.stop // STRIPE]
            nc.vector.tensor_tensor(picked[:], y[b][:].indirect(offsets), gates[r][:, toks], MULT)
            for c in range(width // P):
                nc.tensor.matmul(
                    total[:, c, :],
                    picked[:, c * P : (c + 1) * P],
                    ident[:],
                    start=(r == 0 and c == 0),
                    stop=(r == TOP - 1 and c == width // P - 1),
                    is_transpose=True,
                )

        def apply_gate(b, chunks, total):
            p0 = b * P // PACK
            nc.vector.tensor_tensor(
                gated[:, chunks, :, p0 : p0 + P // PACK],
                total[:].rearrange("p c (q t) -> p c t q", t=PACK),
                og[b][:, chunks, :, :],
                MULT,
            )

        for pair in range(2):
            gather_words(pair, EARLY_TOKENS + 2 * pair * QUARTER)
            gather_scales(pair, EARLY_TOKENS + (2 * pair + 1) * QUARTER)
        for step in range(E + 2):
            if step < E:
                cast_w1(step)
            else:
                cast_w2(1, 0, UNIT, "slot0", (2 * (step - E), 2 * (step - E) + 1), nc.vector.tensor_copy)
            if step >= 2:
                quantize_h(step - 2)
            if step < E:
                quantize_w1(step)
            if 1 <= step <= UNIT:
                gather = gather_words if step % 2 == 1 else gather_scales
                gather(2 + (step - 1) // 2, step * ROOM + 3 * QUARTER)
            if 1 <= step <= E:
                e = step - 1
                cast_w2(0, e - e % 2, 2, "pair%d" % (e // 2 % 2), (e % 2,), nc.scalar.copy)
                first_layer(e)
            if step >= 3 and step % 2 == 1:
                second_layer(0, step - 3, 2, "codes%d" % ((step - 3) // 2 % 2))
                keep_y(0, step - 3, 2)

        for e in range(E):
            load_w2(e, 2)
        cast_w2(1, UNIT, UNIT, "slot2", range(UNIT), nc.scalar.copy)

        gated = keep.tile([P, CHUNKS, PACK, P], F32, name="gated")
        totals = {}
        for b in range(BLOCKS - 1):
            totals[b] = bank(4 + b % 2, [P, CHUNKS, P])
            for half in range(2):
                second_layer(b + 1, UNIT * half, UNIT, "slot%d" % (2 * half + 1))
                if b == 0 and half == 0:
                    for e in range(E):
                        load_w2(e, 3)
                pick(b, 2 * half, slice(0, T), totals[b])
                pick(b, 2 * half + 1, slice(0, T), totals[b])
                keep_y(b + 1, UNIT * half, UNIT)
                if half == 0 and b > 0:
                    output_gate(b - 1, 6 + b % 2, "before_og%d" % (b - 1))
                    apply_gate(b - 1, slice(0, CHUNKS), totals[b - 1])
                if b + 2 < BLOCKS:
                    cast_w2(b + 2, UNIT * half, UNIT, "slot%d" % (2 * half), range(UNIT), nc.scalar.copy)
        output_gate(BLOCKS - 2, 3, "og2")
        output_gate(BLOCKS - 1, 2, "og3")

        result = keep.tile([P, PACK, T], F32, name="result")
        rounded = keep.tile([P, T, PACK], BF16, name="rounded", align_bytes=64)
        codes = keep.tile([P, T], I32, name="codes", align_bytes=64)
        scales = keep.tile([P, T], U8, name="scales", align_bytes=64)
        out_rows = out_0.rearrange("(p t) k -> p t k", t=PACK)
        out_words = out_1[0].rearrange("p k d -> p (k d)").bitcast(I32)

        def turn_back(c, index):
            turned = bank(index, [P, PACK, P])
            for t in range(PACK):
                nc.tensor.transpose(turned[:, t, :], gated[:, c, t, :], ident[:])
            return turned

        last = BLOCKS - 1
        for i, (c0, c1) in enumerate(LAST_RANGES):
            toks = slice(c0 * P, c1 * P)
            total = bank((6, 7, 5)[i], [P, c1 - c0, P])
            for r in range(TOP):
                pick(last, r, toks, total)
                if i == 0 and r == 0:
                    apply_gate(last - 1, slice(0, CHUNKS), totals[last - 1])
            apply_gate(last, slice(c0, c1), total)
            for c in range(c0, c1):
                chunk = slice(c * P, (c + 1) * P)
                turned = turn_back(c, c)
                if c + 1 < CHUNKS:
                    nc.scalar.copy(out=result[:, :, chunk], in_=turned[:])
                    nc.scalar.copy(out=rounded[:, chunk, :], in_=turned[:].rearrange("p t k -> p k t"))
                else:
                    nc.vector.tensor_copy(out=rounded[:, chunk, :], in_=turned[:].rearrange("p t k -> p k t"))
                    nc.scalar.copy(out=result[:, :, chunk], in_=turn_back(c, 0)[:])
                nc.sync.dma_start(out=out_rows[:, :, chunk], in_=result[:, :, chunk])
            nc.vector.quantize_mx(
                out=codes[:, toks].bitcast(FP8X4),
                scales=scales[:, toks],
                in_=rounded[:, toks, :].rearrange("p k t -> p (k t)"),
            )
            nc.sync.dma_start(out=out_words[:, toks], in_=codes[:, toks])
        for quad in range(4):
            nc.sync.dma_start(
                out=out_2[0, 4 * quad : 4 * quad + 4, :].bitcast(I32),
                in_=scales[:].bitcast(I32)[32 * quad : 32 * quad + 4, :],
            )
